import numpy as np
import ml_dtypes


def mxq(x, axis, fmt="e4m3"):
    dtype, down = {"e4m3": (ml_dtypes.float8_e4m3fn, 7), "e5m2": (ml_dtypes.float8_e5m2, 14)}[fmt]
    v = np.moveaxis(np.asarray(x, np.float32).astype(ml_dtypes.bfloat16).astype(np.float64), axis, -1)
    blocks = v.reshape(v.shape[:-1] + (-1, 32))
    amax = np.abs(blocks).max(-1, keepdims=True)
    byte = np.maximum(np.where(amax > 0, np.frexp(amax)[1] - 1 + 127, 0) - down, 1)
    scale = np.exp2(byte - 127.0)
    codes = (blocks / scale).astype(np.float32).astype(dtype).astype(np.float64)
    return np.moveaxis((codes * scale).reshape(v.shape), -1, axis)


WIDE = False


def mx_kscale(k):
    if not WIDE:
        return np.ones(k)
    levels = np.array([10, -10, 5, -5, 0])
    if k % 512:
        return np.exp2(np.random.permutation(np.resize(levels, k // 32))).repeat(32)
    a = np.empty((k // 512, 16))
    for p in range(k // 512):
        a[p, :8] = np.random.permutation(np.resize(levels, 8))
        for g in range(8):
            far = levels[np.abs(levels - a[p, g]) >= 10]
            a[p, g + 8] = far[np.random.randint(len(far))]
    return np.exp2(a.ravel()).repeat(32)


def f64(x):
    return np.asarray(x).astype(np.float64)


def striped(idx):
    return np.tile(np.asarray(idx).reshape(-1, 16).T, (8, 1)).astype(np.uint16)


def unstriped(offs):
    return offs[:16].T.reshape(-1).astype(np.int64)


E2M1 = np.array([0.0, 0.5, 1.0, 1.5, 2.0, 3.0, 4.0, 6.0, -0.0, -0.5, -1.0, -1.5, -2.0, -3.0, -4.0, -6.0])


def pack_weight(w, fmt):
    k, n = w.shape
    w = f64(np.asarray(w, np.float32).astype(ml_dtypes.bfloat16)).reshape(k // 32, 32, n)
    amax = np.abs(w).max(1)
    if fmt == "e4m3":
        byte = np.frexp(amax)[1] - 1 + 127 - 7
    else:
        mant, ex = np.frexp(amax / 6.0)
        byte = np.where(mant > 0.5, ex, ex - 1) + 127
    byte = np.clip(np.where(amax > 0, byte, 1), 1, 254)
    scaled = (w * np.exp2(127.0 - byte)[:, None, :]).reshape(k, n).astype(np.float32)
    by_word = np.ascontiguousarray(scaled.reshape(k // 512, 128, 4, n).transpose(0, 1, 3, 2))
    if fmt == "e4m3":
        words = by_word.astype(ml_dtypes.float8_e4m3fn).view(np.uint8)
    else:
        c = by_word.astype(ml_dtypes.float4_e2m1fn).view(np.uint8) & 0xF
        words = (c[..., 0::2] | (c[..., 1::2] << 4)).reshape(k // 512, 128, 2 * n)
    return np.ascontiguousarray(words), np.ascontiguousarray(byte.astype(np.uint8).reshape(k // 512, 16, n))


def unpack_weight(words, scales, fmt):
    g, _, n = scales.shape
    words = np.ascontiguousarray(words).reshape(g, 128, n, -1)
    if fmt == "e4m3":
        vals = words.view(ml_dtypes.float8_e4m3fn).astype(np.float64)
    else:
        nib = np.empty((g, 128, n, 4), np.uint8)
        nib[..., 0::2] = words & 0xF
        nib[..., 1::2] = words >> 4
        vals = E2M1[nib]
    vals = vals * np.repeat(np.exp2(scales.astype(np.float64) - 127.0), 8, axis=1)[..., None]
    return vals.transpose(0, 1, 3, 2).reshape(g * 512, n)


D, E, T, I, Q = 512, 512, 2048, 512, 128


def setup_inputs():
    n = np.random.standard_normal
    idx = np.random.permutation(T)[:I]
    fd = mx_kscale(D)
    fi = mx_kscale(I)
    ti = np.ones(T)
    ti[idx] = fi
    keysp = pack_weight(n((D, T)) / fd[:, None], "e2m1")
    return {
        "query": (n((D, Q)) * 1.0 / np.sqrt(D) * fd[:, None]).astype(np.float32),
        "keys_words": keysp[0],
        "keys_scales": keysp[1],
        "sharp": (np.random.uniform(0.4, 1.0, (Q, 1))).astype(np.float32),
        "os": (np.random.uniform(4.0, 16.0, (1, I)) * fi).astype(np.float32),
        "vals": (n((E, T)) / ti).astype(np.float32),
        "offs": striped(idx),
    }


def reference(query, keys_words, keys_scales, sharp, os, vals, offs):
    idx = unstriped(offs)
    keysu = unpack_weight(keys_words, keys_scales, "e2m1")
    queryq = mxq(f64(query), 0, "e4m3")
    keysidxg = keysu[:, idx]
    a = queryq.T @ keysidxg
    m1 = np.mean(a, axis=1, keepdims=True)
    ce = a - m1
    sd = np.sqrt(np.mean(np.square(ce), axis=1, keepdims=True) + 0.05)
    s = ce / sd * f64(sharp)
    p = np.exp(s - np.max(s, axis=1, keepdims=True))
    z = np.sum(p, axis=1, keepdims=True)
    w = p / z
    wo1 = w * f64(os)
    wt1 = wo1.T
    vt1 = f64(vals)[:, idx].T
    wt1q = mxq(wt1, 0, "e4m3")
    vt1q = mxq(vt1, 0, "e4m3")
    o = wt1q.T @ vt1q
    return o

@@ -1,0 +1,198 @@
+from contextlib import ExitStack
+
+import concourse.mybir as mybir
+from concourse.masks import make_identity
+
+D, E, T, I, Q = 512, 512, 2048, 512, 128
+P = 128
+PACK = 4
+EPS = 0.05
+
+F32 = mybir.dt.float32
+BF16 = mybir.dt.bfloat16
+I32 = mybir.dt.int32
+U32 = mybir.dt.uint32
+U16 = mybir.dt.uint16
+U8 = mybir.dt.uint8
+FP8X4 = mybir.dt.float8_e4m3fn_x4
+FP4X4 = mybir.dt.float4_e2m1fn_x4
+ALU = mybir.AluOpType
+ACT = mybir.ActivationFunctionType
+
+FLOPS = 2 * Q * D * I + 2 * Q * I * E
+
+
+def tile_attend_standardised_kernel(tc, query, keys_words, keys_scales, sharp, slot_factor, vals, offs, out):
+    nc = tc.nc
+    chunks = E // P
+
+    with ExitStack() as ctx:
+        sb = ctx.enter_context(tc.tile_pool(name="sb", bufs=1))
+        big = ctx.enter_context(tc.tile_pool(name="big", bufs=1))
+        ps = ctx.enter_context(tc.psum_pool(name="ps", bufs=1))
+
+        offsets = sb.tile([P, I // 16], U16, name="offsets")
+        nc.sync.dma_start(offsets[:], offs)
+
+        scale_pool = sb.tile([P, T], U8, name="scale_pool")
+        nc.gpsimd.memset(scale_pool[:].bitcast(I32), 0)
+        for quad in range(4):
+            nc.sync.dma_start(
+                scale_pool[32 * quad : 32 * quad + 4, :].bitcast(I32),
+                keys_scales[0, 4 * quad : 4 * quad + 4, :].bitcast(I32),
+            )
+
+        key_pool = sb.tile([P, T], U16, name="key_pool")
+        nc.sync.dma_start(key_pool[:].bitcast(I32), keys_words[0].bitcast(I32))
+
+        q_raw = sb.tile([P, PACK, Q], F32, name="q_raw")
+        nc.sync.dma_start(q_raw[:], query.rearrange("(p j) q -> p j q", j=PACK))
+
+        row = sb.tile([P, 8], F32, name="row")
+        os_cols = sb.tile([P, PACK], F32, name="os_cols")
+        val_pools = []
+        for c in range(chunks):
+            val_pool = big.tile([P, T], F32, name="val_pool%d" % c, offset=c * T * 4, align_bytes=64)
+            nc.sync.dma_start(val_pool[:], vals[c * P : (c + 1) * P, :])
+            val_pools.append(val_pool)
+            if c == 0:
+                nc.sync.dma_start(row[:, 4:5], sharp)
+                nc.sync.dma_start(os_cols[:], slot_factor.rearrange("o (p t) -> p (o t)", t=PACK))
+
+        ident = sb.tile([P, P], F32, name="ident")
+        make_identity(nc, ident[:])
+        minus_half = sb.tile([P, 1], F32, name="minus_half")
+        nc.gpsimd.memset(minus_half[:], -0.5)
+
+        warm = sb.tile([P, 1], F32, name="warm")
+        nc.scalar.activation(warm[:], minus_half[:], ACT.Exp)
+
+        q_bf = sb.tile([P, Q, PACK], BF16, name="q_bf", align_bytes=64)
+        nc.scalar.copy(q_bf[:], q_raw[:].rearrange("p j q -> p q j"))
+
+        key_scales = sb.tile([P, I], U8, name="key_scales", align_bytes=64)
+        nc.vector.tensor_copy(key_scales[:], scale_pool[:].indirect(offsets[:]))
+        key_words = sb.tile([P, I], U16, name="key_words", align_bytes=64)
+        nc.vector.tensor_copy(key_words[:], key_pool[:].indirect(offsets[:]))
+
+        q_codes = sb.tile([P, Q], U32, name="q_codes", align_bytes=64)
+        q_scales = sb.tile([P, Q], U8, name="q_scales", align_bytes=64)
+        nc.vector.quantize_mx(q_codes[:].bitcast(FP8X4), q_scales[:], q_bf[:].rearrange("p q j -> p (q j)"))
+
+        os_rows = ps.tile([P, PACK, P], F32, name="os_rows")
+        for t in range(PACK):
+            nc.tensor.transpose(os_rows[:, t, :], os_cols[:, t : t + 1].to_broadcast([P, P]), ident[:])
+
+        scores = ps.tile([Q, I], F32, name="scores")
+        nc.tensor.matmul_mx(
+            scores[:],
+            lhsT=q_codes[:].bitcast(FP8X4),
+            lhsT_scale=q_scales[:],
+            rhs=key_words[:].bitcast(FP4X4),
+            rhs_scale=key_scales[:],
+            start=True,
+            stop=True,
+        )
+
+        picked = [None] * chunks
+
+        def gather(c):
+            picked[c] = sb.tile([P, I], BF16, name="picked%d" % c)
+            nc.vector.tensor_copy(picked[c][:], val_pools[c][:].indirect(offsets[:]))
+
+        def behind(c, slot, shape, dtype, name):
+            return big.tile(shape, dtype, name=name, offset=c * T * 4 + slot * 512, align_bytes=64)
+
+        gather(0)
+        negated = sb.tile([Q, I], F32, name="negated")
+        neg_sum = sb.tile([Q, 1], F32, name="neg_sum")
+        nc.scalar.activation(negated[:], scores[:], ACT.Copy, scale=-1.0, accum_out=neg_sum[:])
+        squares = sb.tile([Q, I], F32, name="squares")
+        sq_sum = sb.tile([Q, 1], F32, name="sq_sum")
+        nc.scalar.activation(
+            squares[:], scores[:], ACT.Square, bias=neg_sum[:], scale=float(I), accum_out=sq_sum[:]
+        )
+        flipped = sb.tile([Q, I], F32, name="flipped")
+        nc.vector.tensor_scalar(
+            flipped[:], negated[:], row[:, 4:5], None, op0=ALU.mult, op1=ALU.min, accum_out=row[:, 0:1]
+        )
+        var_eps = sb.tile([Q, 1], F32, name="var_eps")
+        nc.gpsimd.tensor_scalar(var_eps[:], sq_sum[:], 1.0 / I**3, EPS, op0=ALU.mult, op1=ALU.add)
+        rstd = sb.tile([Q, 1], F32, name="rstd")
+        nc.gpsimd.tensor_tensor(rstd[:], var_eps[:], minus_half[:], ALU.pow)
+        bias_scale = sb.tile([Q, 2], F32, name="bias_scale")
+        nc.scalar.activation(bias_scale[:], row[:, 0:8:4], ACT.Copy, scale=rstd[:])
+
+        p_num = sb.tile([Q, I], F32, name="p_num")
+        z = sb.tile([Q, 1], F32, name="z")
+        nc.scalar.activation(
+            p_num[:], scores[:], ACT.Exp, bias=bias_scale[:, 0:1], scale=bias_scale[:, 1:2], accum_out=z[:]
+        )
+        gather(1)
+        rz = behind(1, 1, [Q, 1], F32, "rz")
+        nc.vector.reciprocal(rz[:], z[:])
+        w_bf = sb.tile([Q, I], BF16, name="w_bf")
+        nc.vector.scalar_tensor_tensor(
+            w_bf[:].rearrange("q (s t) -> q s t", t=PACK),
+            p_num[:].rearrange("q (s t) -> q s t", t=PACK),
+            rz[:],
+            os_rows[:].rearrange("q t s -> q s t"),
+            op0=ALU.mult,
+            op1=ALU.mult,
+        )
+
+        def turn(src, name, bank):
+            words = src[:].bitcast(F32)
+            turned = ps.tile([P, 2, P], F32, name="turned_" + bank)
+            for u in range(2):
+                nc.tensor.transpose(turned[:, u, :], words[:, u : I // 2 : 2], ident[:])
+            grouped = sb.tile([P, I], BF16, name="grouped_" + name, align_bytes=64)
+            nc.scalar.copy(
+                grouped[:].bitcast(F32).rearrange("p (x u) -> p x u", u=2),
+                turned[:].rearrange("p u x -> p x u"),
+            )
+            return grouped
+
+        def quantize(grouped, name, c, slot):
+            codes = behind(c, slot, [P, P], U32, "codes_" + name)
+            scales = sb.tile([P, P], U8, name="scales_" + name, align_bytes=64)
+            nc.vector.quantize_mx(codes[:].bitcast(FP8X4), scales[:], grouped[:])
+            return codes, scales
+
+        early = ps.tile([Q, (chunks - 1) * P], F32, name="early")
+        late = ps.tile([Q, P], F32, name="late")
+
+        def multiply(c, v):
+            acc = late[:] if c == chunks - 1 else early[:, c * P : (c + 1) * P]
+            nc.tensor.matmul_mx(
+                acc,
+                lhsT=w_codes[:].bitcast(FP8X4),
+                lhsT_scale=w_scales[:],
+                rhs=v[0][:].bitcast(FP8X4),
+                rhs_scale=v[1][:],
+                start=True,
+                stop=True,
+            )
+
+        g0 = turn(picked[0], "v0", "v0")
+        g1 = turn(picked[1], "v1", "v1")
+        v0 = quantize(g0, "v0", 1, 0)
+        gw = turn(w_bf, "w", "w")
+        gather(2)
+        g2 = turn(picked[2], "v2", "v0")
+        v1 = quantize(g1, "v1", 2, 0)
+        w_codes, w_scales = quantize(gw, "w", 2, 1)
+        multiply(0, v0)
+        multiply(1, v1)
+        gather(3)
+        g3 = turn(picked[3], "v3", "v1")
+        v2 = quantize(g2, "v2", 3, 0)
+        multiply(2, v2)
+        v3 = quantize(g3, "v3", 3, 1)
+        multiply(3, v3)
+        res_early = sb.tile([Q, (chunks - 1) * P], F32, name="res_early")
+        nc.scalar.copy(res_early[:], early[:])
+        nc.sync.dma_start(out[:, : (chunks - 1) * P], res_early[:])
+        res_late = sb.tile([Q, P], F32, name="res_late")
+        nc.scalar.copy(res_late[:], late[:])
+        nc.sync.dma_start(out[:, (chunks - 1) * P :], res_late[:])

@@ -25,11 +25,15 @@ FLOPS = 2 * Q * D * I + 2 * Q * I * E
 def tile_attend_standardised_kernel(tc, query, keys_words, keys_scales, sharp, slot_factor, vals, offs, out):
     nc = tc.nc
     chunks = E // P
+    SPARE = chunks * (T * 4 + I * 2)
 
     with ExitStack() as ctx:
         sb = ctx.enter_context(tc.tile_pool(name="sb", bufs=1))
         big = ctx.enter_context(tc.tile_pool(name="big", bufs=1))
         ps = ctx.enter_context(tc.psum_pool(name="ps", bufs=1))
+
+        key_pool = sb.tile([P, T], U16, name="key_pool")
+        nc.sync.dma_start(key_pool[:].bitcast(I32), keys_words[0].bitcast(I32))
 
         offsets = sb.tile([P, I // 16], U16, name="offsets")
         nc.sync.dma_start(offsets[:], offs)
@@ -42,13 +46,10 @@ def tile_attend_standardised_kernel(tc, query, keys_words, keys_scales, sharp, s
                 keys_scales[0, 4 * quad : 4 * quad + 4, :].bitcast(I32),
             )
 
-        key_pool = sb.tile([P, T], U16, name="key_pool")
-        nc.sync.dma_start(key_pool[:].bitcast(I32), keys_words[0].bitcast(I32))
-
         q_raw = sb.tile([P, PACK, Q], F32, name="q_raw")
         nc.sync.dma_start(q_raw[:], query.rearrange("(p j) q -> p j q", j=PACK))
 
-        row = sb.tile([P, 8], F32, name="row")
+        sharp_col = sb.tile([P, 1], F32, name="sharp_col")
         os_cols = sb.tile([P, PACK], F32, name="os_cols")
         val_pools = []
         for c in range(chunks):
@@ -56,7 +57,7 @@ def tile_attend_standardised_kernel(tc, query, keys_words, keys_scales, sharp, s
             nc.sync.dma_start(val_pool[:], vals[c * P : (c + 1) * P, :])
             val_pools.append(val_pool)
             if c == 0:
-                nc.sync.dma_start(row[:, 4:5], sharp)
+                nc.sync.dma_start(sharp_col[:], sharp)
                 nc.sync.dma_start(os_cols[:], slot_factor.rearrange("o (p t) -> p (o t)", t=PACK))
 
         ident = sb.tile([P, P], F32, name="ident")
@@ -79,10 +80,6 @@ def tile_attend_standardised_kernel(tc, query, keys_words, keys_scales, sharp, s
         q_scales = sb.tile([P, Q], U8, name="q_scales", align_bytes=64)
         nc.vector.quantize_mx(q_codes[:].bitcast(FP8X4), q_scales[:], q_bf[:].rearrange("p q j -> p (q j)"))
 
-        os_rows = ps.tile([P, PACK, P], F32, name="os_rows")
-        for t in range(PACK):
-            nc.tensor.transpose(os_rows[:, t, :], os_cols[:, t : t + 1].to_broadcast([P, P]), ident[:])
-
         scores = ps.tile([Q, I], F32, name="scores")
         nc.tensor.matmul_mx(
             scores[:],
@@ -94,59 +91,28 @@ def tile_attend_standardised_kernel(tc, query, keys_words, keys_scales, sharp, s
             stop=True,
         )
 
+        os_rows = ps.tile([P, PACK, P], F32, name="os_rows")
+        for t in range(PACK):
+            nc.tensor.transpose(os_rows[:, t, :], os_cols[:, t : t + 1].to_broadcast([P, P]), ident[:])
+
         picked = [None] * chunks
 
         def gather(c):
-            picked[c] = sb.tile([P, I], BF16, name="picked%d" % c)
+            picked[c] = big.tile([P, I], BF16, name="picked%d" % c, offset=chunks * T * 4 + c * I * 2, align_bytes=64)
             nc.vector.tensor_copy(picked[c][:], val_pools[c][:].indirect(offsets[:]))
 
         def behind(c, slot, shape, dtype, name):
             return big.tile(shape, dtype, name=name, offset=c * T * 4 + slot * 512, align_bytes=64)
-
-        gather(0)
-        negated = sb.tile([Q, I], F32, name="negated")
-        neg_sum = sb.tile([Q, 1], F32, name="neg_sum")
-        nc.scalar.activation(negated[:], scores[:], ACT.Copy, scale=-1.0, accum_out=neg_sum[:])
-        squares = sb.tile([Q, I], F32, name="squares")
-        sq_sum = sb.tile([Q, 1], F32, name="sq_sum")
-        nc.scalar.activation(
-            squares[:], scores[:], ACT.Square, bias=neg_sum[:], scale=float(I), accum_out=sq_sum[:]
-        )
-        flipped = sb.tile([Q, I], F32, name="flipped")
-        nc.vector.tensor_scalar(
-            flipped[:], negated[:], row[:, 4:5], None, op0=ALU.mult, op1=ALU.min, accum_out=row[:, 0:1]
-        )
-        var_eps = sb.tile([Q, 1], F32, name="var_eps")
-        nc.gpsimd.tensor_scalar(var_eps[:], sq_sum[:], 1.0 / I**3, EPS, op0=ALU.mult, op1=ALU.add)
-        rstd = sb.tile([Q, 1], F32, name="rstd")
-        nc.gpsimd.tensor_tensor(rstd[:], var_eps[:], minus_half[:], ALU.pow)
-        bias_scale = sb.tile([Q, 2], F32, name="bias_scale")
-        nc.scalar.activation(bias_scale[:], row[:, 0:8:4], ACT.Copy, scale=rstd[:])
-
-        p_num = sb.tile([Q, I], F32, name="p_num")
-        z = sb.tile([Q, 1], F32, name="z")
-        nc.scalar.activation(
-            p_num[:], scores[:], ACT.Exp, bias=bias_scale[:, 0:1], scale=bias_scale[:, 1:2], accum_out=z[:]
-        )
-        gather(1)
-        rz = behind(1, 1, [Q, 1], F32, "rz")
-        nc.vector.reciprocal(rz[:], z[:])
-        w_bf = sb.tile([Q, I], BF16, name="w_bf")
-        nc.vector.scalar_tensor_tensor(
-            w_bf[:].rearrange("q (s t) -> q s t", t=PACK),
-            p_num[:].rearrange("q (s t) -> q s t", t=PACK),
-            rz[:],
-            os_rows[:].rearrange("q t s -> q s t"),
-            op0=ALU.mult,
-            op1=ALU.mult,
-        )
 
         def turn(src, name, bank):
             words = src[:].bitcast(F32)
             turned = ps.tile([P, 2, P], F32, name="turned_" + bank)
             for u in range(2):
                 nc.tensor.transpose(turned[:, u, :], words[:, u : I // 2 : 2], ident[:])
-            grouped = sb.tile([P, I], BF16, name="grouped_" + name, align_bytes=64)
+            if name == "v0":
+                grouped = big.tile([P, I], BF16, name="grouped_" + name, offset=SPARE, align_bytes=64)
+            else:
+                grouped = sb.tile([P, I], BF16, name="grouped_" + name, align_bytes=64)
             nc.scalar.copy(
                 grouped[:].bitcast(F32).rearrange("p (x u) -> p x u", u=2),
                 turned[:].rearrange("p u x -> p x u"),
@@ -158,6 +124,45 @@ def tile_attend_standardised_kernel(tc, query, keys_words, keys_scales, sharp, s
             scales = sb.tile([P, P], U8, name="scales_" + name, align_bytes=64)
             nc.vector.quantize_mx(codes[:].bitcast(FP8X4), scales[:], grouped[:])
             return codes, scales
+
+        gather(0)
+        negated = sb.tile([Q, I], F32, name="negated")
+        neg_sum = sb.tile([Q, 1], F32, name="neg_sum")
+        nc.scalar.activation(negated[:], scores[:], ACT.Copy, scale=-1.0, accum_out=neg_sum[:])
+        squares = sb.tile([Q, I], F32, name="squares")
+        sq_sum = sb.tile([Q, 1], F32, name="sq_sum")
+        nc.scalar.activation(
+            squares[:], scores[:], ACT.Square, bias=neg_sum[:], scale=float(I), accum_out=sq_sum[:]
+        )
+        neg_max = sb.tile([Q, 1], F32, name="neg_max")
+        flipped = behind(0, 0, [Q, I], F32, "flipped")
+        nc.vector.tensor_scalar(
+            flipped[:], negated[:], sharp_col[:], None, op0=ALU.mult, op1=ALU.min, accum_out=neg_max[:]
+        )
+        shifted = sb.tile([Q, I], F32, name="shifted")
+        nc.vector.tensor_scalar(shifted[:], flipped[:], neg_max[:], -1.0, op0=ALU.subtract, op1=ALU.mult)
+        var_eps = sb.tile([Q, 1], F32, name="var_eps")
+        nc.scalar.activation(var_eps[:], sq_sum[:], ACT.Copy, scale=1.0 / I**3, bias=EPS)
+        rstd = big.tile([Q, 1], F32, name="rstd", offset=SPARE, align_bytes=64)
+        nc.gpsimd.tensor_tensor(rstd[:], var_eps[:], minus_half[:], ALU.pow)
+
+        p_num = sb.tile([Q, I], F32, name="p_num")
+        z = sb.tile([Q, 1], F32, name="z")
+        nc.scalar.activation(p_num[:], shifted[:], ACT.Exp, scale=rstd[:], accum_out=z[:])
+        gather(1)
+        rz = behind(1, 1, [Q, 1], F32, "rz")
+        nc.vector.reciprocal(rz[:], z[:])
+        g0 = turn(picked[0], "v0", "v0")
+        v0 = quantize(g0, "v0", 1, 0)
+        w_bf = sb.tile([Q, I], BF16, name="w_bf")
+        nc.vector.scalar_tensor_tensor(
+            w_bf[:].rearrange("q (s t) -> q s t", t=PACK),
+            p_num[:].rearrange("q (s t) -> q s t", t=PACK),
+            rz[:],
+            os_rows[:].rearrange("q t s -> q s t"),
+            op0=ALU.mult,
+            op1=ALU.mult,
+        )
 
         early = ps.tile([Q, (chunks - 1) * P], F32, name="early")
         late = ps.tile([Q, P], F32, name="late")
@@ -174,19 +179,17 @@ def tile_attend_standardised_kernel(tc, query, keys_words, keys_scales, sharp, s
                 stop=True,
             )
 
-        g0 = turn(picked[0], "v0", "v0")
         g1 = turn(picked[1], "v1", "v1")
-        v0 = quantize(g0, "v0", 1, 0)
         gw = turn(w_bf, "w", "w")
         gather(2)
         g2 = turn(picked[2], "v2", "v0")
-        v1 = quantize(g1, "v1", 2, 0)
-        w_codes, w_scales = quantize(gw, "w", 2, 1)
-        multiply(0, v0)
-        multiply(1, v1)
         gather(3)
         g3 = turn(picked[3], "v3", "v1")
+        w_codes, w_scales = quantize(gw, "w", 3, 2)
+        v1 = quantize(g1, "v1", 3, 3)
         v2 = quantize(g2, "v2", 3, 0)
+        multiply(0, v0)
+        multiply(1, v1)
         multiply(2, v2)
         v3 = quantize(g3, "v3", 3, 1)
         multiply(3, v3)

@@ -65,9 +65,6 @@ def tile_attend_standardised_kernel(tc, query, keys_words, keys_scales, sharp, s
         minus_half = sb.tile([P, 1], F32, name="minus_half")
         nc.gpsimd.memset(minus_half[:], -0.5)
 
-        warm = sb.tile([P, 1], F32, name="warm")
-        nc.scalar.activation(warm[:], minus_half[:], ACT.Exp)
-
         q_bf = sb.tile([P, Q, PACK], BF16, name="q_bf", align_bytes=64)
         nc.scalar.copy(q_bf[:], q_raw[:].rearrange("p j q -> p q j"))
 
@@ -150,19 +147,18 @@ def tile_attend_standardised_kernel(tc, query, keys_words, keys_scales, sharp, s
         z = sb.tile([Q, 1], F32, name="z")
         nc.scalar.activation(p_num[:], shifted[:], ACT.Exp, scale=rstd[:], accum_out=z[:])
         gather(1)
-        rz = behind(1, 1, [Q, 1], F32, "rz")
+        p_os = behind(1, 1, [Q, I], F32, "p_os")
+        nc.vector.tensor_tensor(
+            p_os[:].rearrange("q (s t) -> q s t", t=PACK),
+            p_num[:].rearrange("q (s t) -> q s t", t=PACK),
+            os_rows[:].rearrange("q t s -> q s t"),
+            ALU.mult,
+        )
+        rz = behind(1, 0, [Q, 1], F32, "rz")
         nc.vector.reciprocal(rz[:], z[:])
         g0 = turn(picked[0], "v0", "v0")
-        v0 = quantize(g0, "v0", 1, 0)
         w_bf = sb.tile([Q, I], BF16, name="w_bf")
-        nc.vector.scalar_tensor_tensor(
-            w_bf[:].rearrange("q (s t) -> q s t", t=PACK),
-            p_num[:].rearrange("q (s t) -> q s t", t=PACK),
-            rz[:],
-            os_rows[:].rearrange("q t s -> q s t"),
-            op0=ALU.mult,
-            op1=ALU.mult,
-        )
+        nc.scalar.activation(w_bf[:], p_os[:], ACT.Copy, scale=rz[:])
 
         early = ps.tile([Q, (chunks - 1) * P], F32, name="early")
         late = ps.tile([Q, P], F32, name="late")
@@ -186,6 +182,7 @@ def tile_attend_standardised_kernel(tc, query, keys_words, keys_scales, sharp, s
         gather(3)
         g3 = turn(picked[3], "v3", "v1")
         w_codes, w_scales = quantize(gw, "w", 3, 2)
+        v0 = quantize(g0, "v0", 3, 4)
         v1 = quantize(g1, "v1", 3, 3)
         v2 = quantize(g2, "v2", 3, 0)
         multiply(0, v0)

from contextlib import ExitStack

import concourse.mybir as mybir
from concourse.masks import make_identity

D, E, T, I, Q = 512, 512, 2048, 512, 128
P = 128
PACK = 4
EPS = 0.05

F32 = mybir.dt.float32
BF16 = mybir.dt.bfloat16
I32 = mybir.dt.int32
U32 = mybir.dt.uint32
U16 = mybir.dt.uint16
U8 = mybir.dt.uint8
FP8X4 = mybir.dt.float8_e4m3fn_x4
FP4X4 = mybir.dt.float4_e2m1fn_x4
ALU = mybir.AluOpType
ACT = mybir.ActivationFunctionType

FLOPS = 2 * Q * D * I + 2 * Q * I * E


def tile_attend_standardised_kernel(tc, query, keys_words, keys_scales, sharp, slot_factor, vals, offs, out):
    nc = tc.nc
    chunks = E // P
    SPARE = chunks * (T * 4 + I * 2)

    with ExitStack() as ctx:
        sb = ctx.enter_context(tc.tile_pool(name="sb", bufs=1))
        big = ctx.enter_context(tc.tile_pool(name="big", bufs=1))
        ps = ctx.enter_context(tc.psum_pool(name="ps", bufs=1))

        key_pool = sb.tile([P, T], U16, name="key_pool")
        nc.sync.dma_start(key_pool[:].bitcast(I32), keys_words[0].bitcast(I32))

        offsets = sb.tile([P, I // 16], U16, name="offsets")
        nc.sync.dma_start(offsets[:], offs)

        scale_pool = sb.tile([P, T], U8, name="scale_pool")
        nc.gpsimd.memset(scale_pool[:].bitcast(I32), 0)
        for quad in range(4):
            nc.sync.dma_start(
                scale_pool[32 * quad : 32 * quad + 4, :].bitcast(I32),
                keys_scales[0, 4 * quad : 4 * quad + 4, :].bitcast(I32),
            )

        q_raw = sb.tile([P, PACK, Q], F32, name="q_raw")
        nc.sync.dma_start(q_raw[:], query.rearrange("(p j) q -> p j q", j=PACK))

        sharp_col = sb.tile([P, 1], F32, name="sharp_col")
        os_cols = sb.tile([P, PACK], F32, name="os_cols")
        val_pools = []
        for c in range(chunks):
            val_pool = big.tile([P, T], F32, name="val_pool%d" % c, offset=c * T * 4, align_bytes=64)
            nc.sync.dma_start(val_pool[:], vals[c * P : (c + 1) * P, :])
            val_pools.append(val_pool)
            if c == 0:
                nc.sync.dma_start(sharp_col[:], sharp)
                nc.sync.dma_start(os_cols[:], slot_factor.rearrange("o (p t) -> p (o t)", t=PACK))

        ident = sb.tile([P, P], F32, name="ident")
        make_identity(nc, ident[:])
        minus_half = sb.tile([P, 1], F32, name="minus_half")
        nc.gpsimd.memset(minus_half[:], -0.5)

        q_bf = sb.tile([P, Q, PACK], BF16, name="q_bf", align_bytes=64)
        nc.scalar.copy(q_bf[:], q_raw[:].rearrange("p j q -> p q j"))

        key_scales = sb.tile([P, I], U8, name="key_scales", align_bytes=64)
        nc.vector.tensor_copy(key_scales[:], scale_pool[:].indirect(offsets[:]))
        key_words = sb.tile([P, I], U16, name="key_words", align_bytes=64)
        nc.vector.tensor_copy(key_words[:], key_pool[:].indirect(offsets[:]))

        q_codes = sb.tile([P, Q], U32, name="q_codes", align_bytes=64)
        q_scales = sb.tile([P, Q], U8, name="q_scales", align_bytes=64)
        nc.vector.quantize_mx(q_codes[:].bitcast(FP8X4), q_scales[:], q_bf[:].rearrange("p q j -> p (q j)"))

        scores = ps.tile([Q, I], F32, name="scores")
        nc.tensor.matmul_mx(
            scores[:],
            lhsT=q_codes[:].bitcast(FP8X4),
            lhsT_scale=q_scales[:],
            rhs=key_words[:].bitcast(FP4X4),
            rhs_scale=key_scales[:],
            start=True,
            stop=True,
        )

        os_rows = ps.tile([P, PACK, P], F32, name="os_rows")
        for t in range(PACK):
            nc.tensor.transpose(os_rows[:, t, :], os_cols[:, t : t + 1].to_broadcast([P, P]), ident[:])

        picked = [None] * chunks

        def gather(c):
            picked[c] = big.tile([P, I], BF16, name="picked%d" % c, offset=chunks * T * 4 + c * I * 2, align_bytes=64)
            nc.vector.tensor_copy(picked[c][:], val_pools[c][:].indirect(offsets[:]))

        def behind(c, slot, shape, dtype, name):
            return big.tile(shape, dtype, name=name, offset=c * T * 4 + slot * 512, align_bytes=64)

        def turn(src, name, bank):
            words = src[:].bitcast(F32)
            turned = ps.tile([P, 2, P], F32, name="turned_" + bank)
            for u in range(2):
                nc.tensor.transpose(turned[:, u, :], words[:, u : I // 2 : 2], ident[:])
            if name == "v0":
                grouped = big.tile([P, I], BF16, name="grouped_" + name, offset=SPARE, align_bytes=64)
            else:
                grouped = sb.tile([P, I], BF16, name="grouped_" + name, align_bytes=64)
            nc.scalar.copy(
                grouped[:].bitcast(F32).rearrange("p (x u) -> p x u", u=2),
                turned[:].rearrange("p u x -> p x u"),
            )
            return grouped

        def quantize(grouped, name, c, slot):
            codes = behind(c, slot, [P, P], U32, "codes_" + name)
            scales = sb.tile([P, P], U8, name="scales_" + name, align_bytes=64)
            nc.vector.quantize_mx(codes[:].bitcast(FP8X4), scales[:], grouped[:])
            return codes, scales

        gather(0)
        negated = sb.tile([Q, I], F32, name="negated")
        neg_sum = sb.tile([Q, 1], F32, name="neg_sum")
        nc.scalar.activation(negated[:], scores[:], ACT.Copy, scale=-1.0, accum_out=neg_sum[:])
        squares = sb.tile([Q, I], F32, name="squares")
        sq_sum = sb.tile([Q, 1], F32, name="sq_sum")
        nc.scalar.activation(
            squares[:], scores[:], ACT.Square, bias=neg_sum[:], scale=float(I), accum_out=sq_sum[:]
        )
        neg_max = sb.tile([Q, 1], F32, name="neg_max")
        flipped = behind(0, 0, [Q, I], F32, "flipped")
        nc.vector.tensor_scalar(
            flipped[:], negated[:], sharp_col[:], None, op0=ALU.mult, op1=ALU.min, accum_out=neg_max[:]
        )
        shifted = sb.tile([Q, I], F32, name="shifted")
        nc.vector.tensor_scalar(shifted[:], flipped[:], neg_max[:], -1.0, op0=ALU.subtract, op1=ALU.mult)
        var_eps = sb.tile([Q, 1], F32, name="var_eps")
        nc.scalar.activation(var_eps[:], sq_sum[:], ACT.Copy, scale=1.0 / I**3, bias=EPS)
        rstd = big.tile([Q, 1], F32, name="rstd", offset=SPARE, align_bytes=64)
        nc.gpsimd.tensor_tensor(rstd[:], var_eps[:], minus_half[:], ALU.pow)

        p_num = sb.tile([Q, I], F32, name="p_num")
        z = sb.tile([Q, 1], F32, name="z")
        nc.scalar.activation(p_num[:], shifted[:], ACT.Exp, scale=rstd[:], accum_out=z[:])
        gather(1)
        p_os = behind(1, 1, [Q, I], F32, "p_os")
        nc.vector.tensor_tensor(
            p_os[:].rearrange("q (s t) -> q s t", t=PACK),
            p_num[:].rearrange("q (s t) -> q s t", t=PACK),
            os_rows[:].rearrange("q t s -> q s t"),
            ALU.mult,
        )
        rz = behind(1, 0, [Q, 1], F32, "rz")
        nc.vector.reciprocal(rz[:], z[:])
        g0 = turn(picked[0], "v0", "v0")
        w_bf = sb.tile([Q, I], BF16, name="w_bf")
        nc.scalar.activation(w_bf[:], p_os[:], ACT.Copy, scale=rz[:])

        early = ps.tile([Q, (chunks - 1) * P], F32, name="early")
        late = ps.tile([Q, P], F32, name="late")

        def multiply(c, v):
            acc = late[:] if c == chunks - 1 else early[:, c * P : (c + 1) * P]
            nc.tensor.matmul_mx(
                acc,
                lhsT=w_codes[:].bitcast(FP8X4),
                lhsT_scale=w_scales[:],
                rhs=v[0][:].bitcast(FP8X4),
                rhs_scale=v[1][:],
                start=True,
                stop=True,
            )

        g1 = turn(picked[1], "v1", "v1")
        gw = turn(w_bf, "w", "w")
        gather(2)
        g2 = turn(picked[2], "v2", "v0")
        gather(3)
        g3 = turn(picked[3], "v3", "v1")
        w_codes, w_scales = quantize(gw, "w", 3, 2)
        v0 = quantize(g0, "v0", 3, 4)
        v1 = quantize(g1, "v1", 3, 3)
        v2 = quantize(g2, "v2", 3, 0)
        multiply(0, v0)
        multiply(1, v1)
        multiply(2, v2)
        v3 = quantize(g3, "v3", 3, 1)
        multiply(3, v3)
        res_early = sb.tile([Q, (chunks - 1) * P], F32, name="res_early")
        nc.scalar.copy(res_early[:], early[:])
        nc.sync.dma_start(out[:, : (chunks - 1) * P], res_early[:])
        res_late = sb.tile([Q, P], F32, name="res_late")
        nc.scalar.copy(res_late[:], late[:])
        nc.sync.dma_start(out[:, (chunks - 1) * P :], res_late[:])
